import numpy as np
import ml_dtypes


def mxq(x, axis, fmt="e4m3"):
    dtype, down = {"e4m3": (ml_dtypes.float8_e4m3fn, 7), "e5m2": (ml_dtypes.float8_e5m2, 14)}[fmt]
    v = np.moveaxis(np.asarray(x, np.float32).astype(ml_dtypes.bfloat16).astype(np.float64), axis, -1)
    blocks = v.reshape(v.shape[:-1] + (-1, 32))
    amax = np.abs(blocks).max(-1, keepdims=True)
    byte = np.maximum(np.where(amax > 0, np.frexp(amax)[1] - 1 + 127, 0) - down, 1)
    scale = np.exp2(byte - 127.0)
    codes = (blocks / scale).astype(np.float32).astype(dtype).astype(np.float64)
    return np.moveaxis((codes * scale).reshape(v.shape), -1, axis)


WIDE = False


def mx_kscale(k):
    if not WIDE:
        return np.ones(k)
    levels = np.array([10, -10, 5, -5, 0])
    if k % 512:
        return np.exp2(np.random.permutation(np.resize(levels, k // 32))).repeat(32)
    a = np.empty((k // 512, 16))
    for p in range(k // 512):
        a[p, :8] = np.random.permutation(np.resize(levels, 8))
        for g in range(8):
            far = levels[np.abs(levels - a[p, g]) >= 10]
            a[p, g + 8] = far[np.random.randint(len(far))]
    return np.exp2(a.ravel()).repeat(32)


def f64(x):
    return np.asarray(x).astype(np.float64)


def striped8(idx):
    return np.concatenate([v.reshape(-1, 16).T for v in idx]).astype(np.uint16)


def unstriped8(offs):
    return np.stack([offs[16 * g:16 * g + 16].T.reshape(-1) for g in range(8)]).astype(np.int64)


K, M, T, S = 1536, 256, 1024, 512


def setup_inputs():
    n = np.random.standard_normal
    s = mx_kscale(K)[:, None]
    return {
        "xT": (n((K, T)) * s).astype(np.float32),
        "w": (n((K, M)) / np.sqrt(K) / s).astype(np.float32),
        "wgt": np.repeat(np.random.uniform(0.5, 2.0, (8, S)), 16, axis=0).astype(np.float32),
        "b": (0.3 * n(256)).astype(np.float32),
        "wgo": np.repeat(np.random.uniform(0.5, 2.0, (8, S)), 16, axis=0).astype(np.float32),
        "offs": striped8(np.stack([np.random.permutation(T)[:S] for _ in range(8)])),
        "offs2": striped8(np.stack([np.random.permutation(T)[:S] for _ in range(8)])),
    }


def reference(xT, w, wgt, b, wgo, offs, offs2):
    idx = unstriped8(offs)
    group = np.arange(K) % 512 // 64
    xg = f64(wgt)[np.arange(K) // 4 % 128] * f64(xT)[np.arange(K)[:, None], idx[group]]
    xT_ = mxq(xg, 0, "e4m3")
    w_ = mxq(f64(w), 0, "e4m3")
    y = w_.T @ xT_
    place = unstriped8(offs2)[np.arange(M) % 128 // 16]
    out = np.zeros((M, T))
    out[np.arange(M)[:, None], place] = f64(wgo)[np.arange(M) % 128] * (y + f64(b)[:, None])
    return out

@@ -1,0 +1,191 @@
+import concourse.mybir as mybir
+
+K, M, T, S = 1536, 256, 1024, 512
+
+F32 = mybir.dt.float32
+BF16 = mybir.dt.bfloat16
+U32 = mybir.dt.uint32
+U16 = mybir.dt.uint16
+U8 = mybir.dt.uint8
+FP8X4 = mybir.dt.float8_e4m3fn_x4
+MULT = mybir.AluOpType.mult
+IDENTITY = mybir.ActivationFunctionType.Identity
+
+P = 128
+PACK = 4
+K_PASS = P * PACK
+PASSES = K // K_PASS
+LAST = PASSES - 1
+M_TILES = M // P
+HALVES = 2
+H = S // HALVES
+HCOLS = H // 16
+
+FLOPS = 2 * K * M * S
+
+
+def tile_list_hboth_bias_kernel(tc, xT, w, wgt, b, wgo, offs, offs2, out):
+    nc = tc.nc
+
+    with (
+        tc.tile_pool(name="keep", bufs=1) as keep,
+        tc.psum_pool(name="psum", bufs=1) as psum,
+    ):
+        idx = keep.tile([P, S // 16], U16, name="idx")
+        idx2 = keep.tile([P, S // 16], U16, name="idx2")
+        wgt_sb = [keep.tile([P, H], F32, name=f"wgt{h}") for h in range(HALVES)]
+        wgo_sb = keep.tile([P, S], F32, name="wgo_sb")
+        b_sb = [keep.tile([P, 1], F32, name=f"b{m}") for m in range(M_TILES)]
+        x_sb = [[keep.tile([P, T], F32, name=f"x{a}_{i}") for i in range(PACK)] for a in range(PASSES)]
+        w_sb = [keep.tile([P, PACK, M], F32, name=f"w{a}") for a in range(PASSES)]
+
+        def load_x(a, i):
+            rows = xT[a * K_PASS : (a + 1) * K_PASS, :].rearrange("(p i) t -> p i t", i=PACK)
+            nc.sync.dma_start(out=x_sb[a][i][:], in_=rows[:, i, :])
+
+        def load_w(a):
+            rows = w[a * K_PASS : (a + 1) * K_PASS, :].rearrange("(p i) n -> p i n", i=PACK)
+            nc.sync.dma_start(out=w_sb[a][:], in_=rows)
+
+        nc.sync.dma_start(out=idx[:], in_=offs)
+        nc.sync.dma_start(out=wgt_sb[0][:], in_=wgt[:, 0:H])
+        load_x(0, 0)
+        nc.sync.dma_start(out=wgt_sb[1][:], in_=wgt[:, H:S])
+        load_x(0, 1)
+        load_x(0, 2)
+        load_x(0, 3)
+        load_x(1, 0)
+        load_x(1, 1)
+        load_w(0)
+        load_x(1, 2)
+        load_x(1, 3)
+        load_x(2, 0)
+        load_w(1)
+        load_x(2, 1)
+        nc.sync.dma_start(out=idx2[:], in_=offs2)
+        load_x(2, 2)
+        load_x(2, 3)
+        load_w(2)
+        nc.sync.dma_start(out=wgo_sb[:], in_=wgo)
+        for m in range(M_TILES):
+            nc.sync.dma_start(out=b_sb[m][:], in_=b[m * P : (m + 1) * P].rearrange("(p o) -> p o", o=1))
+
+        placed = [keep.tile([P, T], F32, name=f"placed{m}") for m in range(M_TILES)]
+        for m in range(M_TILES):
+            nc.vector.memset(placed[m][:], 0.0)
+
+        g_sb = [[keep.tile([P, PACK, H], F32, name=f"g{a}_{h}") for h in range(HALVES)] for a in range(PASSES)]
+        x_bf = [keep.tile([P, S, PACK], BF16, name=f"xbf{a}", align_bytes=64) for a in range(PASSES)]
+        x_codes = [keep.tile([P, S], U32, name=f"xc{a}", align_bytes=64) for a in range(PASSES)]
+        x_scales = [keep.tile([P, S], U8, name=f"xs{a}", align_bytes=64) for a in range(PASSES)]
+        w_bf = [keep.tile([P, M, PACK], BF16, name=f"wbf{a}", align_bytes=64) for a in range(PASSES)]
+        w_codes = [keep.tile([P, M], U32, name=f"wc{a}", align_bytes=64) for a in range(PASSES)]
+        w_scales = [keep.tile([P, M], U8, name=f"ws{a}", align_bytes=64) for a in range(PASSES)]
+        acc = [[psum.tile([P, H], F32, name=f"acc{m}_{h}") for h in range(HALVES)] for m in range(M_TILES)]
+        y_sb = [[keep.tile([P, H], F32, name=f"y{m}_{h}") for h in range(HALVES)] for m in range(M_TILES)]
+
+        def gather(a, i, h):
+            nc.vector.tensor_tensor(
+                g_sb[a][h][:, i, :],
+                x_sb[a][i][:].indirect(idx[:, h * HCOLS : (h + 1) * HCOLS]),
+                wgt_sb[h][:],
+                MULT,
+            )
+
+        def interleave_x(a, h):
+            nc.scalar.copy(out=x_bf[a][:, h * H : (h + 1) * H, :], in_=g_sb[a][h][:].rearrange("p i j -> p j i"))
+
+        def interleave_w(a):
+            nc.scalar.copy(out=w_bf[a][:], in_=w_sb[a][:].rearrange("p i n -> p n i"))
+
+        def quantize_x(a, lo, hi):
+            nc.vector.quantize_mx(
+                out=x_codes[a][:, lo:hi].bitcast(FP8X4),
+                scales=x_scales[a][:, lo:hi],
+                in_=x_bf[a][:].rearrange("p j i -> p (j i)")[:, PACK * lo : PACK * hi],
+            )
+
+        def quantize_w(a):
+            nc.vector.quantize_mx(
+                out=w_codes[a][:].bitcast(FP8X4),
+                scales=w_scales[a][:],
+                in_=w_bf[a][:].rearrange("p n i -> p (n i)"),
+            )
+
+        def multiply(a, m, h):
+            js, ns = slice(h * H, (h + 1) * H), slice(m * P, (m + 1) * P)
+            nc.tensor.matmul_mx(
+                out=acc[m][h][:],
+                lhsT=w_codes[a][:, ns].bitcast(FP8X4),
+                lhsT_scale=w_scales[a][:, ns],
+                rhs=x_codes[a][:, js].bitcast(FP8X4),
+                rhs_scale=x_scales[a][:, js],
+                start=(a == 0),
+                stop=(a == LAST),
+            )
+
+        def add_bias(m, h):
+            nc.scalar.activation(out=y_sb[m][h][:], in_=acc[m][h][:], func=IDENTITY, bias=b_sb[m][:])
+
+        def scatter(m, h):
+            nc.vector.tensor_tensor(
+                placed[m][:].indirect(idx2[:, h * HCOLS : (h + 1) * HCOLS]),
+                y_sb[m][h][:],
+                wgo_sb[:, h * H : (h + 1) * H],
+                MULT,
+            )
+
+        def multiply_pass(a):
+            for m in range(M_TILES):
+                for h in range(HALVES):
+                    multiply(a, m, h)
+
+        for i in range(PACK):
+            for h in range(HALVES):
+                gather(0, i, h)
+        for h in range(HALVES):
+            interleave_x(0, h)
+        for i in range(2):
+            for h in range(HALVES):
+                gather(1, i, h)
+        quantize_x(0, 0, S)
+        interleave_w(0)
+        for i in range(2, PACK):
+            for h in range(HALVES):
+                gather(1, i, h)
+        for h in range(HALVES):
+            interleave_x(1, h)
+        quantize_w(0)
+        multiply_pass(0)
+
+        gather(2, 0, 0)
+        gather(2, 0, 1)
+        interleave_w(1)
+        gather(2, 1, 0)
+        gather(2, 1, 1)
+        quantize_x(1, 0, S)
+        quantize_w(1)
+        multiply_pass(1)
+        gather(2, 2, 0)
+        gather(2, 3, 0)
+        interleave_x(2, 0)
+        interleave_w(2)
+        gather(2, 2, 1)
+        gather(2, 3, 1)
+        quantize_x(2, 0, H)
+        quantize_w(2)
+        for m in range(M_TILES):
+            multiply(2, m, 0)
+        add_bias(0, 0)
+        interleave_x(2, 1)
+        scatter(0, 0)
+        add_bias(1, 0)
+        quantize_x(2, H, S)
+        for m in range(M_TILES):
+            multiply(2, m, 1)
+        scatter(1, 0)
+        for m in range(M_TILES):
+            add_bias(m, 1)
+        for m in range(M_TILES):
+            scatter(m, 1)
+            nc.sync.dma_start(out=out[m * P : (m + 1) * P, :], in_=placed[m][:])

@@ -62,10 +62,10 @@ def tile_list_hboth_bias_kernel(tc, xT, w, wgt, b, wgo, offs, offs2, out):
         load_x(2, 0)
         load_w(1)
         load_x(2, 1)
-        nc.sync.dma_start(out=idx2[:], in_=offs2)
         load_x(2, 2)
-        load_x(2, 3)
         load_w(2)
+        load_x(2, 3)
+        nc.sync.dma_start(out=idx2[:], in_=offs2)
         nc.sync.dma_start(out=wgo_sb[:], in_=wgo)
         for m in range(M_TILES):
             nc.sync.dma_start(out=b_sb[m][:], in_=b[m * P : (m + 1) * P].rearrange("(p o) -> p o", o=1))
@@ -92,11 +92,14 @@ def tile_list_hboth_bias_kernel(tc, xT, w, wgt, b, wgo, offs, offs2, out):
                 MULT,
             )
 
-        def interleave_x(a, h):
-            nc.scalar.copy(out=x_bf[a][:, h * H : (h + 1) * H, :], in_=g_sb[a][h][:].rearrange("p i j -> p j i"))
+        def interleave_x(a, h, lo=0, hi=H):
+            nc.scalar.copy(
+                out=x_bf[a][:, h * H + lo : h * H + hi, :],
+                in_=g_sb[a][h][:, :, lo:hi].rearrange("p i j -> p j i"),
+            )
 
-        def interleave_w(a):
-            nc.scalar.copy(out=w_bf[a][:], in_=w_sb[a][:].rearrange("p i n -> p n i"))
+        def interleave_w(a, lo=0, hi=M):
+            nc.scalar.copy(out=w_bf[a][:, lo:hi, :], in_=w_sb[a][:, :, lo:hi].rearrange("p i n -> p n i"))
 
         def quantize_x(a, lo, hi):
             nc.vector.quantize_mx(
@@ -105,11 +108,11 @@ def tile_list_hboth_bias_kernel(tc, xT, w, wgt, b, wgo, offs, offs2, out):
                 in_=x_bf[a][:].rearrange("p j i -> p (j i)")[:, PACK * lo : PACK * hi],
             )
 
-        def quantize_w(a):
+        def quantize_w(a, lo=0, hi=M):
             nc.vector.quantize_mx(
-                out=w_codes[a][:].bitcast(FP8X4),
-                scales=w_scales[a][:],
-                in_=w_bf[a][:].rearrange("p n i -> p (n i)"),
+                out=w_codes[a][:, lo:hi].bitcast(FP8X4),
+                scales=w_scales[a][:, lo:hi],
+                in_=w_bf[a][:].rearrange("p n i -> p (n i)")[:, PACK * lo : PACK * hi],
             )
 
         def multiply(a, m, h):
@@ -158,28 +161,28 @@ def tile_list_hboth_bias_kernel(tc, xT, w, wgt, b, wgo, offs, offs2, out):
         quantize_w(0)
         multiply_pass(0)
 
-        gather(2, 0, 0)
-        gather(2, 0, 1)
+        for i in range(2):
+            for h in range(HALVES):
+                gather(2, i, h)
         interleave_w(1)
-        gather(2, 1, 0)
-        gather(2, 1, 1)
+        gather(2, 2, 0)
         quantize_x(1, 0, S)
+        gather(2, 2, 1)
+        interleave_w(2)
         quantize_w(1)
         multiply_pass(1)
-        gather(2, 2, 0)
         gather(2, 3, 0)
         interleave_x(2, 0)
-        interleave_w(2)
-        gather(2, 2, 1)
+        quantize_w(2)
         gather(2, 3, 1)
         quantize_x(2, 0, H)
-        quantize_w(2)
         for m in range(M_TILES):
             multiply(2, m, 0)
         add_bias(0, 0)
-        interleave_x(2, 1)
-        scatter(0, 0)
+        interleave_x(2, 1, 0, H // 2)
         add_bias(1, 0)
+        interleave_x(2, 1, H // 2, H)
+        scatter(0, 0)
         quantize_x(2, H, S)
         for m in range(M_TILES):
             multiply(2, m, 1)

@@ -74,39 +74,56 @@ def tile_list_hboth_bias_kernel(tc, xT, w, wgt, b, wgo, offs, offs2, out):
         for m in range(M_TILES):
             nc.vector.memset(placed[m][:], 0.0)
 
-        g_sb = [[keep.tile([P, PACK, H], F32, name=f"g{a}_{h}") for h in range(HALVES)] for a in range(PASSES)]
-        x_bf = [keep.tile([P, S, PACK], BF16, name=f"xbf{a}", align_bytes=64) for a in range(PASSES)]
-        x_codes = [keep.tile([P, S], U32, name=f"xc{a}", align_bytes=64) for a in range(PASSES)]
-        x_scales = [keep.tile([P, S], U8, name=f"xs{a}", align_bytes=64) for a in range(PASSES)]
-        w_bf = [keep.tile([P, M, PACK], BF16, name=f"wbf{a}", align_bytes=64) for a in range(PASSES)]
+        held = {"xbf2_0": "late", "g2_384": "late", "y1_0": "late"}
+
+        def new_tile(shape, dtype, name):
+            return keep.tile(shape, dtype, name=name, tag=held.get(name, name), align_bytes=64)
+
+        g_sb = {}
+        w_bf = {}
         w_codes = [keep.tile([P, M], U32, name=f"wc{a}", align_bytes=64) for a in range(PASSES)]
         w_scales = [keep.tile([P, M], U8, name=f"ws{a}", align_bytes=64) for a in range(PASSES)]
         acc = [[psum.tile([P, H], F32, name=f"acc{m}_{h}") for h in range(HALVES)] for m in range(M_TILES)]
-        y_sb = [[keep.tile([P, H], F32, name=f"y{m}_{h}") for h in range(HALVES)] for m in range(M_TILES)]
+        y_sb = {}
 
-        def gather(a, i, h):
+        def gather(a, i, lo, hi):
+            if (a, lo) not in g_sb:
+                g_sb[a, lo] = new_tile([P, PACK, hi - lo], F32, f"g{a}_{lo}")
             nc.vector.tensor_tensor(
-                g_sb[a][h][:, i, :],
-                x_sb[a][i][:].indirect(idx[:, h * HCOLS : (h + 1) * HCOLS]),
-                wgt_sb[h][:],
+                g_sb[a, lo][:, i, :],
+                x_sb[a][i][:].indirect(idx[:, lo // 16 : hi // 16]),
+                wgt_sb[lo // H][:, lo % H : lo % H + hi - lo],
                 MULT,
             )
 
-        def interleave_x(a, h, lo=0, hi=H):
-            nc.scalar.copy(
-                out=x_bf[a][:, h * H + lo : h * H + hi, :],
-                in_=g_sb[a][h][:, :, lo:hi].rearrange("p i j -> p j i"),
+        x_bf, x_codes, x_scales = {}, {}, {}
+
+        def interleave_x(a, lo, hi, vector_from=None):
+            mid = hi if vector_from is None else vector_from
+            x_bf[a, lo] = new_tile([P, hi - lo, PACK], BF16, f"xbf{a}_{lo}")
+            for copy, c0, c1 in ((nc.scalar.copy, lo, mid), (nc.vector.tensor_copy, mid, hi)):
+                if c0 < c1:
+                    copy(
+                        out=x_bf[a, lo][:, c0 - lo : c1 - lo, :],
+                        in_=g_sb[a, lo][:, :, c0 - lo : c1 - lo].rearrange("p i j -> p j i"),
+                    )
+
+        def quantize_x(a, lo, hi):
+            h = lo // H
+            if (a, h) not in x_codes:
+                x_codes[a, h] = new_tile([P, H], U32, f"xc{a}_{h}")
+                x_scales[a, h] = new_tile([P, H], U8, f"xs{a}_{h}")
+            js = slice(lo % H, lo % H + hi - lo)
+            nc.vector.quantize_mx(
+                out=x_codes[a, h][:, js].bitcast(FP8X4),
+                scales=x_scales[a, h][:, js],
+                in_=x_bf[a, lo][:].rearrange("p j i -> p (j i)"),
             )
 
         def interleave_w(a, lo=0, hi=M):
+            if a not in w_bf:
+                w_bf[a] = new_tile([P, M, PACK], BF16, f"wbf{a}")
             nc.scalar.copy(out=w_bf[a][:, lo:hi, :], in_=w_sb[a][:, :, lo:hi].rearrange("p i n -> p n i"))
-
-        def quantize_x(a, lo, hi):
-            nc.vector.quantize_mx(
-                out=x_codes[a][:, lo:hi].bitcast(FP8X4),
-                scales=x_scales[a][:, lo:hi],
-                in_=x_bf[a][:].rearrange("p j i -> p (j i)")[:, PACK * lo : PACK * hi],
-            )
 
         def quantize_w(a, lo=0, hi=M):
             nc.vector.quantize_mx(
@@ -116,24 +133,25 @@ def tile_list_hboth_bias_kernel(tc, xT, w, wgt, b, wgo, offs, offs2, out):
             )
 
         def multiply(a, m, h):
-            js, ns = slice(h * H, (h + 1) * H), slice(m * P, (m + 1) * P)
+            ns = slice(m * P, (m + 1) * P)
             nc.tensor.matmul_mx(
                 out=acc[m][h][:],
                 lhsT=w_codes[a][:, ns].bitcast(FP8X4),
                 lhsT_scale=w_scales[a][:, ns],
-                rhs=x_codes[a][:, js].bitcast(FP8X4),
-                rhs_scale=x_scales[a][:, js],
+                rhs=x_codes[a, h][:].bitcast(FP8X4),
+                rhs_scale=x_scales[a, h][:],
                 start=(a == 0),
                 stop=(a == LAST),
             )
 
         def add_bias(m, h):
-            nc.scalar.activation(out=y_sb[m][h][:], in_=acc[m][h][:], func=IDENTITY, bias=b_sb[m][:])
+            y_sb[m, h] = new_tile([P, H], F32, f"y{m}_{h}")
+            nc.scalar.activation(out=y_sb[m, h][:], in_=acc[m][h][:], func=IDENTITY, bias=b_sb[m][:])
 
         def scatter(m, h):
             nc.vector.tensor_tensor(
                 placed[m][:].indirect(idx2[:, h * HCOLS : (h + 1) * HCOLS]),
-                y_sb[m][h][:],
+                y_sb[m, h][:],
                 wgo_sb[:, h * H : (h + 1) * H],
                 MULT,
             )
@@ -143,47 +161,53 @@ def tile_list_hboth_bias_kernel(tc, xT, w, wgt, b, wgo, offs, offs2, out):
                 for h in range(HALVES):
                     multiply(a, m, h)
 
+        A, B, B1, B2 = (0, 256), (256, 512), (256, 384), (384, 512)
         for i in range(PACK):
-            for h in range(HALVES):
-                gather(0, i, h)
-        for h in range(HALVES):
-            interleave_x(0, h)
+            gather(0, i, *A)
+            gather(0, i, *B)
+        interleave_x(0, *A)
+        interleave_x(0, *B)
         for i in range(2):
-            for h in range(HALVES):
-                gather(1, i, h)
-        quantize_x(0, 0, S)
+            gather(1, i, *A)
+            gather(1, i, *B)
+        quantize_x(0, *A)
+        quantize_x(0, *B)
         interleave_w(0)
         for i in range(2, PACK):
-            for h in range(HALVES):
-                gather(1, i, h)
-        for h in range(HALVES):
-            interleave_x(1, h)
+            gather(1, i, *A)
+            gather(1, i, *B)
+        interleave_x(1, *A)
+        interleave_x(1, *B)
         quantize_w(0)
         multiply_pass(0)
 
         for i in range(2):
-            for h in range(HALVES):
-                gather(2, i, h)
+            gather(2, i, *A)
+            gather(2, i, *B1)
         interleave_w(1)
-        gather(2, 2, 0)
-        quantize_x(1, 0, S)
-        gather(2, 2, 1)
+        gather(2, 2, *A)
+        gather(2, 2, *B1)
+        quantize_x(1, *A)
+        quantize_x(1, *B)
         interleave_w(2)
         quantize_w(1)
         multiply_pass(1)
-        gather(2, 3, 0)
-        interleave_x(2, 0)
+        gather(2, 3, *A)
+        interleave_x(2, *A, 128)
         quantize_w(2)
-        gather(2, 3, 1)
-        quantize_x(2, 0, H)
+        gather(2, 3, *B1)
+        quantize_x(2, *A)
         for m in range(M_TILES):
             multiply(2, m, 0)
         add_bias(0, 0)
-        interleave_x(2, 1, 0, H // 2)
-        add_bias(1, 0)
-        interleave_x(2, 1, H // 2, H)
+        interleave_x(2, *B1)
+        for i in range(PACK):
+            gather(2, i, *B2)
+        interleave_x(2, *B2)
         scatter(0, 0)
-        quantize_x(2, H, S)
+        add_bias(1, 0)
+        quantize_x(2, *B1)
+        quantize_x(2, *B2)
         for m in range(M_TILES):
             multiply(2, m, 1)
         scatter(1, 0)

import concourse.mybir as mybir

K, M, T, S = 1536, 256, 1024, 512

F32 = mybir.dt.float32
BF16 = mybir.dt.bfloat16
U32 = mybir.dt.uint32
U16 = mybir.dt.uint16
U8 = mybir.dt.uint8
FP8X4 = mybir.dt.float8_e4m3fn_x4
MULT = mybir.AluOpType.mult
IDENTITY = mybir.ActivationFunctionType.Identity

P = 128
PACK = 4
K_PASS = P * PACK
PASSES = K // K_PASS
LAST = PASSES - 1
M_TILES = M // P
HALVES = 2
H = S // HALVES
HCOLS = H // 16

FLOPS = 2 * K * M * S


def tile_list_hboth_bias_kernel(tc, xT, w, wgt, b, wgo, offs, offs2, out):
    nc = tc.nc

    with (
        tc.tile_pool(name="keep", bufs=1) as keep,
        tc.psum_pool(name="psum", bufs=1) as psum,
    ):
        idx = keep.tile([P, S // 16], U16, name="idx")
        idx2 = keep.tile([P, S // 16], U16, name="idx2")
        wgt_sb = [keep.tile([P, H], F32, name=f"wgt{h}") for h in range(HALVES)]
        wgo_sb = keep.tile([P, S], F32, name="wgo_sb")
        b_sb = [keep.tile([P, 1], F32, name=f"b{m}") for m in range(M_TILES)]
        x_sb = [[keep.tile([P, T], F32, name=f"x{a}_{i}") for i in range(PACK)] for a in range(PASSES)]
        w_sb = [keep.tile([P, PACK, M], F32, name=f"w{a}") for a in range(PASSES)]

        def load_x(a, i):
            rows = xT[a * K_PASS : (a + 1) * K_PASS, :].rearrange("(p i) t -> p i t", i=PACK)
            nc.sync.dma_start(out=x_sb[a][i][:], in_=rows[:, i, :])

        def load_w(a):
            rows = w[a * K_PASS : (a + 1) * K_PASS, :].rearrange("(p i) n -> p i n", i=PACK)
            nc.sync.dma_start(out=w_sb[a][:], in_=rows)

        nc.sync.dma_start(out=idx[:], in_=offs)
        nc.sync.dma_start(out=wgt_sb[0][:], in_=wgt[:, 0:H])
        load_x(0, 0)
        nc.sync.dma_start(out=wgt_sb[1][:], in_=wgt[:, H:S])
        load_x(0, 1)
        load_x(0, 2)
        load_x(0, 3)
        load_x(1, 0)
        load_x(1, 1)
        load_w(0)
        load_x(1, 2)
        load_x(1, 3)
        load_x(2, 0)
        load_w(1)
        load_x(2, 1)
        load_x(2, 2)
        load_w(2)
        load_x(2, 3)
        nc.sync.dma_start(out=idx2[:], in_=offs2)
        nc.sync.dma_start(out=wgo_sb[:], in_=wgo)
        for m in range(M_TILES):
            nc.sync.dma_start(out=b_sb[m][:], in_=b[m * P : (m + 1) * P].rearrange("(p o) -> p o", o=1))

        placed = [keep.tile([P, T], F32, name=f"placed{m}") for m in range(M_TILES)]
        for m in range(M_TILES):
            nc.vector.memset(placed[m][:], 0.0)

        held = {"xbf2_0": "late", "g2_384": "late", "y1_0": "late"}

        def new_tile(shape, dtype, name):
            return keep.tile(shape, dtype, name=name, tag=held.get(name, name), align_bytes=64)

        g_sb = {}
        w_bf = {}
        w_codes = [keep.tile([P, M], U32, name=f"wc{a}", align_bytes=64) for a in range(PASSES)]
        w_scales = [keep.tile([P, M], U8, name=f"ws{a}", align_bytes=64) for a in range(PASSES)]
        acc = [[psum.tile([P, H], F32, name=f"acc{m}_{h}") for h in range(HALVES)] for m in range(M_TILES)]
        y_sb = {}

        def gather(a, i, lo, hi):
            if (a, lo) not in g_sb:
                g_sb[a, lo] = new_tile([P, PACK, hi - lo], F32, f"g{a}_{lo}")
            nc.vector.tensor_tensor(
                g_sb[a, lo][:, i, :],
                x_sb[a][i][:].indirect(idx[:, lo // 16 : hi // 16]),
                wgt_sb[lo // H][:, lo % H : lo % H + hi - lo],
                MULT,
            )

        x_bf, x_codes, x_scales = {}, {}, {}

        def interleave_x(a, lo, hi, vector_from=None):
            mid = hi if vector_from is None else vector_from
            x_bf[a, lo] = new_tile([P, hi - lo, PACK], BF16, f"xbf{a}_{lo}")
            for copy, c0, c1 in ((nc.scalar.copy, lo, mid), (nc.vector.tensor_copy, mid, hi)):
                if c0 < c1:
                    copy(
                        out=x_bf[a, lo][:, c0 - lo : c1 - lo, :],
                        in_=g_sb[a, lo][:, :, c0 - lo : c1 - lo].rearrange("p i j -> p j i"),
                    )

        def quantize_x(a, lo, hi):
            h = lo // H
            if (a, h) not in x_codes:
                x_codes[a, h] = new_tile([P, H], U32, f"xc{a}_{h}")
                x_scales[a, h] = new_tile([P, H], U8, f"xs{a}_{h}")
            js = slice(lo % H, lo % H + hi - lo)
            nc.vector.quantize_mx(
                out=x_codes[a, h][:, js].bitcast(FP8X4),
                scales=x_scales[a, h][:, js],
                in_=x_bf[a, lo][:].rearrange("p j i -> p (j i)"),
            )

        def interleave_w(a, lo=0, hi=M):
            if a not in w_bf:
                w_bf[a] = new_tile([P, M, PACK], BF16, f"wbf{a}")
            nc.scalar.copy(out=w_bf[a][:, lo:hi, :], in_=w_sb[a][:, :, lo:hi].rearrange("p i n -> p n i"))

        def quantize_w(a, lo=0, hi=M):
            nc.vector.quantize_mx(
                out=w_codes[a][:, lo:hi].bitcast(FP8X4),
                scales=w_scales[a][:, lo:hi],
                in_=w_bf[a][:].rearrange("p n i -> p (n i)")[:, PACK * lo : PACK * hi],
            )

        def multiply(a, m, h):
            ns = slice(m * P, (m + 1) * P)
            nc.tensor.matmul_mx(
                out=acc[m][h][:],
                lhsT=w_codes[a][:, ns].bitcast(FP8X4),
                lhsT_scale=w_scales[a][:, ns],
                rhs=x_codes[a, h][:].bitcast(FP8X4),
                rhs_scale=x_scales[a, h][:],
                start=(a == 0),
                stop=(a == LAST),
            )

        def add_bias(m, h):
            y_sb[m, h] = new_tile([P, H], F32, f"y{m}_{h}")
            nc.scalar.activation(out=y_sb[m, h][:], in_=acc[m][h][:], func=IDENTITY, bias=b_sb[m][:])

        def scatter(m, h):
            nc.vector.tensor_tensor(
                placed[m][:].indirect(idx2[:, h * HCOLS : (h + 1) * HCOLS]),
                y_sb[m, h][:],
                wgo_sb[:, h * H : (h + 1) * H],
                MULT,
            )

        def multiply_pass(a):
            for m in range(M_TILES):
                for h in range(HALVES):
                    multiply(a, m, h)

        A, B, B1, B2 = (0, 256), (256, 512), (256, 384), (384, 512)
        for i in range(PACK):
            gather(0, i, *A)
            gather(0, i, *B)
        interleave_x(0, *A)
        interleave_x(0, *B)
        for i in range(2):
            gather(1, i, *A)
            gather(1, i, *B)
        quantize_x(0, *A)
        quantize_x(0, *B)
        interleave_w(0)
        for i in range(2, PACK):
            gather(1, i, *A)
            gather(1, i, *B)
        interleave_x(1, *A)
        interleave_x(1, *B)
        quantize_w(0)
        multiply_pass(0)

        for i in range(2):
            gather(2, i, *A)
            gather(2, i, *B1)
        interleave_w(1)
        gather(2, 2, *A)
        gather(2, 2, *B1)
        quantize_x(1, *A)
        quantize_x(1, *B)
        interleave_w(2)
        quantize_w(1)
        multiply_pass(1)
        gather(2, 3, *A)
        interleave_x(2, *A, 128)
        quantize_w(2)
        gather(2, 3, *B1)
        quantize_x(2, *A)
        for m in range(M_TILES):
            multiply(2, m, 0)
        add_bias(0, 0)
        interleave_x(2, *B1)
        for i in range(PACK):
            gather(2, i, *B2)
        interleave_x(2, *B2)
        scatter(0, 0)
        add_bias(1, 0)
        quantize_x(2, *B1)
        quantize_x(2, *B2)
        for m in range(M_TILES):
            multiply(2, m, 1)
        scatter(1, 0)
        for m in range(M_TILES):
            add_bias(m, 1)
        for m in range(M_TILES):
            scatter(m, 1)
            nc.sync.dma_start(out=out[m * P : (m + 1) * P, :], in_=placed[m][:])
